import numpy as np
import ml_dtypes


def mxq(x, axis, fmt="e4m3"):
    dtype, down = {"e4m3": (ml_dtypes.float8_e4m3fn, 7), "e5m2": (ml_dtypes.float8_e5m2, 14)}[fmt]
    v = np.moveaxis(np.asarray(x, np.float32).astype(ml_dtypes.bfloat16).astype(np.float64), axis, -1)
    blocks = v.reshape(v.shape[:-1] + (-1, 32))
    amax = np.abs(blocks).max(-1, keepdims=True)
    byte = np.maximum(np.where(amax > 0, np.frexp(amax)[1] - 1 + 127, 0) - down, 1)
    scale = np.exp2(byte - 127.0)
    codes = (blocks / scale).astype(np.float32).astype(dtype).astype(np.float64)
    return np.moveaxis((codes * scale).reshape(v.shape), -1, axis)


WIDE = False


def mx_kscale(k):
    if not WIDE:
        return np.ones(k)
    levels = np.array([10, -10, 5, -5, 0])
    if k % 512:
        return np.exp2(np.random.permutation(np.resize(levels, k // 32))).repeat(32)
    a = np.empty((k // 512, 16))
    for p in range(k // 512):
        a[p, :8] = np.random.permutation(np.resize(levels, 8))
        for g in range(8):
            far = levels[np.abs(levels - a[p, g]) >= 10]
            a[p, g + 8] = far[np.random.randint(len(far))]
    return np.exp2(a.ravel()).repeat(32)


def f64(x):
    return np.asarray(x).astype(np.float64)


def striped(idx):
    return np.tile(idx.reshape(-1, 16).T, (8, 1)).astype(np.uint16)


def unstriped(offs):
    return offs[:16].T.reshape(-1).astype(np.int64)


E2M1 = np.array([0.0, 0.5, 1.0, 1.5, 2.0, 3.0, 4.0, 6.0, -0.0, -0.5, -1.0, -1.5, -2.0, -3.0, -4.0, -6.0])


def pack_weight(w, fmt):
    k, n = w.shape
    w = f64(np.asarray(w, np.float32).astype(ml_dtypes.bfloat16)).reshape(k // 32, 32, n)
    amax = np.abs(w).max(1)
    if fmt == "e4m3":
        byte = np.frexp(amax)[1] - 1 + 127 - 7
    else:
        mant, ex = np.frexp(amax / 6.0)
        byte = np.where(mant > 0.5, ex, ex - 1) + 127
    byte = np.clip(np.where(amax > 0, byte, 1), 1, 254)
    scaled = (w * np.exp2(127.0 - byte)[:, None, :]).reshape(k, n).astype(np.float32)
    by_word = np.ascontiguousarray(scaled.reshape(k // 512, 128, 4, n).transpose(0, 1, 3, 2))
    if fmt == "e4m3":
        words = by_word.astype(ml_dtypes.float8_e4m3fn).view(np.uint8)
    else:
        c = by_word.astype(ml_dtypes.float4_e2m1fn).view(np.uint8) & 0xF
        words = (c[..., 0::2] | (c[..., 1::2] << 4)).reshape(k // 512, 128, 2 * n)
    return np.ascontiguousarray(words), np.ascontiguousarray(byte.astype(np.uint8).reshape(k // 512, 16, n))


def unpack_weight(words, scales, fmt):
    g, _, n = scales.shape
    words = np.ascontiguousarray(words).reshape(g, 128, n, -1)
    if fmt == "e4m3":
        vals = words.view(ml_dtypes.float8_e4m3fn).astype(np.float64)
    else:
        nib = np.empty((g, 128, n, 4), np.uint8)
        nib[..., 0::2] = words & 0xF
        nib[..., 1::2] = words >> 4
        vals = E2M1[nib]
    vals = vals * np.repeat(np.exp2(scales.astype(np.float64) - 127.0), 8, axis=1)[..., None]
    return vals.transpose(0, 1, 3, 2).reshape(g * 512, n)


def gelu(v):
    return 0.5 * v * (1.0 + np.tanh(np.sqrt(2.0 / np.pi) * (v + 0.044715 * v**3)))


K, H, T, S, T3, S2, P = 1024, 512, 4096, 1024, 2048, 1024, 512

def setup_inputs():
    n = np.random.standard_normal
    s = mx_kscale(K)[:, None]
    u = mx_kscale(H)[:, None]
    tab_words, tab_scales = pack_weight(n((K, T)) * s, "e4m3")
    tab2_words, tab2_scales = pack_weight(n((H, T3)) / np.sqrt(H) / u, "e4m3")
    w4_words, w4_scales = pack_weight(n((K, H)) / np.sqrt(K) / s * u.T, "e2m1")
    return {
        "tab_words": tab_words, "tab_scales": tab_scales,
        "tab2_words": tab2_words, "tab2_scales": tab2_scales,
        "offs": striped(np.random.permutation(T)[:S]),
        "offs2": striped(np.random.permutation(T3)[:S2]),
        "pos1": striped(np.random.permutation(S)[:P]),
        "pos2": striped(np.random.permutation(S)[:P]),
        "w1": (1.5 * n((K, H)) / np.sqrt(K) / s).astype(np.float32),
        "w4_words": w4_words, "w4_scales": w4_scales,
        "gain": (np.random.uniform(0.4, 1.0, H) * u[:, 0]).astype(np.float32),
        "skip": np.random.uniform(0.3, 0.9, H).astype(np.float32),
        "slope": np.random.uniform(1, 3, S2).astype(np.float32),
        "share": np.random.uniform(0.1, 0.5, S2).astype(np.float32),
        "ref": (0.8 * n((S2, P))).astype(np.float32),
        "rac": np.random.uniform(1.0, 4.0, S2).astype(np.float32),
    }

def reference(tab_words, tab_scales, tab2_words, tab2_scales, offs, offs2, pos1, pos2,
              w1, w4_words, w4_scales, gain, skip, slope, share, ref, rac):
    v = unpack_weight(tab_words, tab_scales, "e4m3")[:, unstriped(offs)]
    v2 = unpack_weight(tab2_words, tab2_scales, "e4m3")[:, unstriped(offs2)]
    w4 = unpack_weight(w4_words, w4_scales, "e2m1")
    z = mxq(f64(w1), 0, "e4m3").T @ v
    res = w4.T @ v
    h = f64(gain)[:, None] * (z / (1.0 + np.exp(-z))) + f64(skip)[:, None] * res
    e = v2.T @ mxq(h, 0, "e4m3")
    top = e.max(axis=1)
    a = 1.0 / (1.0 + np.exp(-f64(slope)[:, None] * (e[:, unstriped(pos1)] - f64(share)[:, None] * top[:, None])))
    c = np.maximum(e[:, unstriped(pos2)], f64(ref))
    return c * a * f64(rac)[:, None]

@@ -1,0 +1,261 @@
+from contextlib import ExitStack
+
+import concourse.mybir as mybir
+from concourse.masks import make_identity
+
+K, H, T, S, T2, S2, NP = 1024, 512, 4096, 1024, 2048, 1024, 512
+FLOPS = 2 * K * H * S * 2 + 2 * H * S2 * S
+
+F32 = mybir.dt.float32
+BF16 = mybir.dt.bfloat16
+I32 = mybir.dt.int32
+U32 = mybir.dt.uint32
+U16 = mybir.dt.uint16
+U8 = mybir.dt.uint8
+FP8X4 = mybir.dt.float8_e4m3fn_x4
+FP4X4 = mybir.dt.float4_e2m1fn_x4
+ALU = mybir.AluOpType
+ACT = mybir.ActivationFunctionType
+AXIS = mybir.AxisListType
+
+P = 128
+PACK = 4
+PASSES = K // (P * PACK)
+BANK = 512
+HALVES = S // BANK
+TILES = S2 // P
+QUADS = 4
+ROWS = 4
+MOVED = 112
+
+
+def tile_list_chiral_column_bench_kernel(
+    tc, tab_words, tab_scales, tab2_words, tab2_scales, offs, offs2, pos1, pos2,
+    w1, w4_words, w4_scales, gain, skip, slope, share, ref, rac, out,
+):
+    nc = tc.nc
+    with ExitStack() as ctx:
+        lists = ctx.enter_context(tc.tile_pool(name="lists", bufs=1))
+        keep = ctx.enter_context(tc.tile_pool(name="keep", bufs=1))
+        ring = ctx.enter_context(tc.tile_pool(name="ring", bufs=4))
+        psum = ctx.enter_context(tc.psum_pool(name="psum", bufs=8))
+
+        def held(shape, dtype, name, tag=None):
+            return keep.tile(shape, dtype, name=name, tag=tag or name, align_bytes=64)
+
+        def bank(name, width=BANK):
+            return psum.tile([P, width], F32, name=name, tag="bank")
+
+        tab_bytes = held([P, T], U8, "tab_bytes", "slot0")
+        nc.vector.memset(tab_bytes[:].bitcast(I32), 0)
+        w4_bytes = held([P, PASSES, H], U8, "w4_bytes")
+        nc.gpsimd.memset(w4_bytes[:].bitcast(I32), 0)
+        tab2_bytes = held([P, T2], U8, "tab2_bytes")
+        nc.vector.memset(tab2_bytes[:].bitcast(I32), 0)
+        v_plane1 = held([P, S], U8, "v_plane1")
+        nc.vector.memset(v_plane1[:].bitcast(I32), 0)
+        row_vectors = held([P, P], F32, "row_vectors")
+        nc.vector.memset(row_vectors[:], 0.0)
+
+        idx = lists.tile([P, S // 16], U16, name="idx")
+        idx2 = lists.tile([P, S2 // 16], U16, name="idx2")
+        p1 = lists.tile([P, NP // 16], U16, name="p1")
+        p2 = lists.tile([P, NP // 16], U16, name="p2")
+        nc.sync.dma_start(idx[:], offs)
+        nc.sync.dma_start(idx2[:], offs2)
+        nc.sync.dma_start(p1[:], pos1)
+        nc.sync.dma_start(p2[:], pos2)
+        w4_raw = held([P, PASSES, 2 * H], U8, "w4_raw", "slot2")
+        nc.scalar.dma_start(w4_raw[:].bitcast(I32), w4_words.rearrange("a p c -> p a c").bitcast(I32))
+        skip_c = held([P, PACK], F32, "skip_c")
+        gain_c = held([P, PACK], F32, "gain_c")
+        nc.scalar.dma_start(skip_c[:], skip.rearrange("(p t) -> p t", t=PACK))
+        nc.scalar.dma_start(gain_c[:], gain.rearrange("(p t) -> p t", t=PACK))
+        for q in range(QUADS):
+            nc.scalar.dma_start(
+                tab_bytes[32 * q : 32 * q + PASSES * ROWS, :].bitcast(I32),
+                tab_scales[:, ROWS * q : ROWS * (q + 1), :].bitcast(I32),
+            )
+        tab_tiles = []
+
+        def load_tab(a):
+            words = held([P, T], U32, "tab%d" % a, "slot%d" % (a + 1))
+            nc.sync.dma_start(words[:].bitcast(I32), tab_words[a].rearrange("p t i -> p (t i)").bitcast(I32))
+            tab_tiles.append(words)
+
+        load_tab(0)
+        for q in range(QUADS):
+            nc.gpsimd.dma_start(
+                w4_bytes[32 * q : 32 * q + ROWS, :, :].bitcast(I32),
+                w4_scales[:, ROWS * q : ROWS * (q + 1), :].rearrange("a r c -> r a c").bitcast(I32),
+            )
+        for q in range(QUADS):
+            nc.scalar.dma_start(
+                tab2_bytes[32 * q : 32 * q + ROWS, :].bitcast(I32),
+                tab2_scales[0, ROWS * q : ROWS * (q + 1), :].bitcast(I32),
+            )
+        for n, vec in enumerate((slope, share, rac)):
+            nc.gpsimd.dma_start(row_vectors[TILES * n : TILES * (n + 1), :], vec.rearrange("(i p) -> i p", p=P))
+        identity = held([P, P], F32, "identity")
+        make_identity(nc, identity[:])
+
+        w4_codes = held([P, PASSES, PACK, 2 * P], U8, "w4_codes")
+        nc.vector.tensor_copy(
+            w4_codes[:].rearrange("p a t (m b) -> p a m t b", b=2),
+            w4_raw[:].rearrange("p a (m t b) -> p a m t b", t=PACK, b=2),
+        )
+        load_tab(1)
+        v_plane0 = held([P, S], U8, "v_plane0")
+        nc.vector.tensor_copy(v_plane0[:], tab_bytes[:].indirect(idx[:]))
+        nc.scalar.dma_start(v_plane1[0:MOVED, :].bitcast(I32), v_plane0[ROWS : ROWS + MOVED, :].bitcast(I32))
+        v_planes = (v_plane0, v_plane1)
+
+        w4_plane = held([P, PASSES, PACK, P], U8, "w4_plane")
+        nc.vector.tensor_copy(
+            w4_plane[:].rearrange("p a t m -> p a m t"),
+            w4_bytes[:].rearrange("p a (m t) -> p a m t", t=PACK),
+        )
+
+        v_words = {}
+
+        def gather_tab(a):
+            for half in range(HALVES):
+                picked = held([P, BANK], U32, "v%d%d" % (a, half))
+                cols = slice(half * BANK // 16, (half + 1) * BANK // 16)
+                nc.vector.tensor_copy(picked[:], tab_tiles[a][:].indirect(idx[:, cols]))
+                v_words[a, half] = picked
+
+        gather_tab(0)
+        v2_plane = held([P, S2], U8, "v2_plane")
+        nc.vector.tensor_copy(v2_plane[:], tab2_bytes[:].indirect(idx2[:]))
+        gather_tab(1)
+
+        w1_raw = []
+        for a in range(PASSES):
+            raw = held([P, PACK, H], F32, "w1_raw%d" % a, "slot%d" % a)
+            nc.sync.dma_start(raw[:], w1[a * P * PACK : (a + 1) * P * PACK, :].rearrange("(p j) c -> p j c", j=PACK))
+            w1_raw.append(raw)
+        tab2_tile = held([P, T2], U32, "tab2", "slot2")
+        nc.sync.dma_start(tab2_tile[:].bitcast(I32), tab2_words[0].rearrange("p t i -> p (t i)").bitcast(I32))
+
+        turned = bank("turned", P)
+        nc.tensor.transpose(turned[:], row_vectors[:], identity[:])
+        col_vectors = held([P, 3 * TILES], F32, "col_vectors")
+        nc.scalar.copy(col_vectors[:], turned[:, 0 : 3 * TILES])
+        gate_factor = held([P, TILES], F32, "gate_factor")
+        nc.vector.scalar_tensor_tensor(
+            gate_factor[:], col_vectors[:, 0:TILES], -1.0, col_vectors[:, TILES : 2 * TILES], ALU.mult, ALU.mult
+        )
+
+        skipped = {}
+        for half in range(HALVES):
+            cols = slice(half * BANK, (half + 1) * BANK)
+            for t in range(PACK):
+                acc = bank("res")
+                for a in range(PASSES):
+                    nc.tensor.matmul_mx(
+                        acc[:], lhsT=w4_codes[:, a, t, :].bitcast(FP4X4), lhsT_scale=w4_plane[:, a, t, :],
+                        rhs=v_words[a, half][:].bitcast(FP8X4), rhs_scale=v_planes[a][:, cols],
+                        start=(a == 0), stop=(a == PASSES - 1),
+                    )
+                res = held([P, BANK], F32, "res%d%d" % (half, t))
+                nc.scalar.activation(res[:], acc[:], ACT.Copy, scale=skip_c[:, t : t + 1])
+                skipped[half, t] = res
+
+        w1_codes, w1_planes = [], []
+        for a in range(PASSES):
+            grouped = held([P, PACK * H], BF16, "w1_grouped%d" % a)
+            nc.vector.tensor_copy(
+                grouped[:].rearrange("p (t m j) -> p m j t", t=PACK, j=PACK),
+                w1_raw[a][:].rearrange("p j (m t) -> p m j t", t=PACK),
+            )
+            codes = held([P, H], U32, "w1_codes%d" % a)
+            plane = held([P, H], U8, "w1_plane%d" % a)
+            nc.vector.quantize_mx(out=codes[:].bitcast(FP8X4), scales=plane[:], in_=grouped[:])
+            w1_codes.append(codes)
+            w1_planes.append(plane)
+
+        ref_tiles = []
+        for a in range(2):
+            given = held([P, TILES // 2, NP], F32, "ref%d" % a, "slot%d" % a)
+            rows = slice(a * S2 // 2, (a + 1) * S2 // 2)
+            nc.sync.dma_start(given[:], ref[rows, :].rearrange("(i p) n -> p i n", p=P))
+            ref_tiles.append(given)
+
+        v2_words = held([P, S2], U32, "v2_words")
+        nc.vector.tensor_copy(v2_words[:], tab2_tile[:].indirect(idx2[:]))
+
+        h_rows, h_grouped = [], []
+        for half in range(HALVES):
+            cols = slice(half * BANK, (half + 1) * BANK)
+            rows4 = held([P, PACK, BANK], BF16, "h_rows%d" % half)
+            for t in range(PACK):
+                acc = bank("z")
+                wcols = slice(t * P, (t + 1) * P)
+                for a in range(PASSES):
+                    nc.tensor.matmul_mx(
+                        acc[:], lhsT=w1_codes[a][:, wcols].bitcast(FP8X4), lhsT_scale=w1_planes[a][:, wcols],
+                        rhs=v_words[a, half][:].bitcast(FP8X4), rhs_scale=v_planes[a][:, cols],
+                        start=(a == 0), stop=(a == PASSES - 1),
+                    )
+                act = ring.tile([P, BANK], F32, name="act")
+                nc.scalar.activation(act[:], acc[:], ACT.Silu)
+                nc.vector.scalar_tensor_tensor(
+                    rows4[:, t, :], act[:], gain_c[:, t : t + 1], skipped[half, t][:], ALU.mult, ALU.add
+                )
+            h_rows.append(rows4)
+
+        h_codes, h_planes = [], []
+        for half in range(HALVES):
+            grouped = held([P, PACK * BANK], BF16, "h_grouped%d" % half)
+            weave = nc.scalar.copy if half == 0 else nc.vector.tensor_copy
+            weave(
+                grouped[:].rearrange("p (c i t) -> p c t i", i=4, t=PACK),
+                h_rows[half][:].rearrange("p t (c i) -> p c t i", i=4),
+            )
+            h_grouped.append(grouped)
+        for half in range(HALVES):
+            codes = held([P, BANK], U32, "h_codes%d" % half)
+            plane = held([P, BANK], U8, "h_plane%d" % half)
+            nc.vector.quantize_mx(out=codes[:].bitcast(FP8X4), scales=plane[:], in_=h_grouped[half][:])
+            h_codes.append(codes)
+            h_planes.append(plane)
+
+        top = held([P, TILES], F32, "top")
+        gate_bias = held([P, TILES], F32, "gate_bias")
+        floors, gates = [], []
+
+        def finish(i):
+            result = ring.tile([P, NP], F32, name="result")
+            nc.vector.scalar_tensor_tensor(
+                result[:], floors[i][:], col_vectors[:, 2 * TILES + i : 2 * TILES + i + 1], gates[i][:], ALU.mult, ALU.mult
+            )
+            nc.sync.dma_start(out[i * P : (i + 1) * P, :], result[:])
+
+        for i in range(TILES):
+            mcols = slice(i * P, (i + 1) * P)
+            col = slice(i, i + 1)
+            scores = ring.tile([P, S], F32, name="scores")
+            for half in range(HALVES):
+                acc = bank("e")
+                nc.tensor.matmul_mx(
+                    acc[:], lhsT=v2_words[:, mcols].bitcast(FP8X4), lhsT_scale=v2_plane[:, mcols],
+                    rhs=h_codes[half][:].bitcast(FP8X4), rhs_scale=h_planes[half][:],
+                    start=True, stop=True,
+                )
+                nc.scalar.copy(scores[:, half * BANK : (half + 1) * BANK], acc[:])
+            nc.vector.tensor_reduce(top[:, col], scores[:], AXIS.X, ALU.max)
+            picked = ring.tile([P, NP], F32, name="picked")
+            nc.vector.tensor_copy(picked[:], scores[:].indirect(p2[:]))
+            nc.scalar.activation(gate_bias[:, col], top[:, col], ACT.Copy, scale=gate_factor[:, col])
+            gate = ring.tile([P, NP], F32, name="gate")
+            nc.scalar.activation(
+                gate[:], scores[:].indirect(p1[:]), ACT.Sigmoid, bias=gate_bias[:, col], scale=col_vectors[:, col]
+            )
+            if i > 0:
+                finish(i - 1)
+            floored = ring.tile([P, NP], F32, name="floored")
+            nc.vector.tensor_tensor(floored[:], picked[:], ref_tiles[i // 4][:, i % 4, :], ALU.max)
+            floors.append(floored)
+            gates.append(gate)
+        finish(TILES - 1)

@@ -26,7 +26,9 @@ HALVES = S // BANK
 TILES = S2 // P
 QUADS = 4
 ROWS = 4
-MOVED = 112
+DEAD = 32 - PASSES * ROWS
+MOVED = 96 + ROWS
+DIRECT = 3
 
 
 def tile_list_chiral_column_bench_kernel(
@@ -46,74 +48,85 @@ def tile_list_chiral_column_bench_kernel(
         def bank(name, width=BANK):
             return psum.tile([P, width], F32, name=name, tag="bank")
 
-        tab_bytes = held([P, T], U8, "tab_bytes", "slot0")
-        nc.vector.memset(tab_bytes[:].bitcast(I32), 0)
+        tab2_bytes = held([P, T2], U8, "tab2_bytes", "slot1")
+        nc.gpsimd.memset(tab2_bytes[:].bitcast(I32), 0)
         w4_bytes = held([P, PASSES, H], U8, "w4_bytes")
         nc.gpsimd.memset(w4_bytes[:].bitcast(I32), 0)
-        tab2_bytes = held([P, T2], U8, "tab2_bytes")
-        nc.vector.memset(tab2_bytes[:].bitcast(I32), 0)
-        v_plane1 = held([P, S], U8, "v_plane1")
-        nc.vector.memset(v_plane1[:].bitcast(I32), 0)
+        tab_bytes = held([P, T], U8, "tab_bytes")
+        for q in range(QUADS):
+            clear = nc.vector.memset if q % 2 else nc.gpsimd.memset
+            clear(tab_bytes[32 * q : 32 * q + DEAD, :].bitcast(I32), 0)
         row_vectors = held([P, P], F32, "row_vectors")
         nc.vector.memset(row_vectors[:], 0.0)
+        v_planes = []
+        for a in range(PASSES):
+            plane = held([P, S], U8, "v_plane%d" % a)
+            nc.vector.memset(plane[96:P, :].bitcast(I32), 0)
+            v_planes.append(plane)
 
         idx = lists.tile([P, S // 16], U16, name="idx")
         idx2 = lists.tile([P, S2 // 16], U16, name="idx2")
         p1 = lists.tile([P, NP // 16], U16, name="p1")
         p2 = lists.tile([P, NP // 16], U16, name="p2")
-        nc.sync.dma_start(idx[:], offs)
-        nc.sync.dma_start(idx2[:], offs2)
-        nc.sync.dma_start(p1[:], pos1)
-        nc.sync.dma_start(p2[:], pos2)
-        w4_raw = held([P, PASSES, 2 * H], U8, "w4_raw", "slot2")
-        nc.scalar.dma_start(w4_raw[:].bitcast(I32), w4_words.rearrange("a p c -> p a c").bitcast(I32))
-        skip_c = held([P, PACK], F32, "skip_c")
-        gain_c = held([P, PACK], F32, "gain_c")
-        nc.scalar.dma_start(skip_c[:], skip.rearrange("(p t) -> p t", t=PACK))
-        nc.scalar.dma_start(gain_c[:], gain.rearrange("(p t) -> p t", t=PACK))
-        for q in range(QUADS):
-            nc.scalar.dma_start(
-                tab_bytes[32 * q : 32 * q + PASSES * ROWS, :].bitcast(I32),
-                tab_scales[:, ROWS * q : ROWS * (q + 1), :].bitcast(I32),
-            )
         tab_tiles = []
 
         def load_tab(a):
-            words = held([P, T], U32, "tab%d" % a, "slot%d" % (a + 1))
+            words = held([P, T], U32, "tab%d" % a, "slot0" if a == 0 else None)
             nc.sync.dma_start(words[:].bitcast(I32), tab_words[a].rearrange("p t i -> p (t i)").bitcast(I32))
             tab_tiles.append(words)
 
-        load_tab(0)
+        w1_raw = []
+
+        def load_w1(a, tag):
+            raw = held([P, PACK, H], F32, "w1_raw%d" % a, tag)
+            nc.sync.dma_start(raw[:], w1[a * P * PACK : (a + 1) * P * PACK, :].rearrange("(p j) c -> p j c", j=PACK))
+            w1_raw.append(raw)
+
+        nc.sync.dma_start(idx[:], offs)
         for q in range(QUADS):
-            nc.gpsimd.dma_start(
-                w4_bytes[32 * q : 32 * q + ROWS, :, :].bitcast(I32),
-                w4_scales[:, ROWS * q : ROWS * (q + 1), :].rearrange("a r c -> r a c").bitcast(I32),
+            nc.sync.dma_start(
+                tab_bytes[32 * q + DEAD : 32 * (q + 1), :].bitcast(I32),
+                tab_scales[:, ROWS * q : ROWS * (q + 1), :].bitcast(I32),
             )
+        w4_raw = held([P, PASSES, 2 * H], U8, "w4_raw")
+        nc.sync.dma_start(w4_raw[:].bitcast(I32), w4_words.rearrange("a p c -> p a c").bitcast(I32))
+        load_tab(0)
+        nc.sync.dma_start(idx2[:], offs2)
         for q in range(QUADS):
-            nc.scalar.dma_start(
+            nc.sync.dma_start(
                 tab2_bytes[32 * q : 32 * q + ROWS, :].bitcast(I32),
                 tab2_scales[0, ROWS * q : ROWS * (q + 1), :].bitcast(I32),
             )
-        for n, vec in enumerate((slope, share, rac)):
-            nc.gpsimd.dma_start(row_vectors[TILES * n : TILES * (n + 1), :], vec.rearrange("(i p) -> i p", p=P))
+        load_w1(0, "slot2")
+        for q in range(QUADS):
+            nc.sync.dma_start(
+                w4_bytes[32 * q : 32 * q + ROWS, :, :].bitcast(I32),
+                w4_scales[:, ROWS * q : ROWS * (q + 1), :].rearrange("a r c -> r a c").bitcast(I32),
+            )
+        load_tab(1)
+        nc.sync.dma_start(p1[:], pos1)
+        nc.sync.dma_start(p2[:], pos2)
+        skip_c = held([P, PACK], F32, "skip_c")
+        gain_c = held([P, PACK], F32, "gain_c")
         identity = held([P, P], F32, "identity")
         make_identity(nc, identity[:])
+        nc.gpsimd.dma_start(skip_c[:], skip.rearrange("(p t) -> p t", t=PACK))
+
+        v_bytes = held([P, S], U8, "v_bytes")
+        nc.vector.tensor_copy(v_bytes[:], tab_bytes[:].indirect(idx[:]))
+        for a in range(PASSES):
+            first = DEAD + a * ROWS
+            nc.gpsimd.dma_start(
+                v_planes[a][0:MOVED, :].bitcast(I32), v_bytes[first : first + MOVED, :].bitcast(I32)
+            )
+        nc.gpsimd.dma_start(gain_c[:], gain.rearrange("(p t) -> p t", t=PACK))
+        for n, vec in enumerate((slope, share, rac)):
+            nc.gpsimd.dma_start(row_vectors[TILES * n : TILES * (n + 1), :], vec.rearrange("(i p) -> i p", p=P))
 
         w4_codes = held([P, PASSES, PACK, 2 * P], U8, "w4_codes")
         nc.vector.tensor_copy(
             w4_codes[:].rearrange("p a t (m b) -> p a m t b", b=2),
             w4_raw[:].rearrange("p a (m t b) -> p a m t b", t=PACK, b=2),
-        )
-        load_tab(1)
-        v_plane0 = held([P, S], U8, "v_plane0")
-        nc.vector.tensor_copy(v_plane0[:], tab_bytes[:].indirect(idx[:]))
-        nc.scalar.dma_start(v_plane1[0:MOVED, :].bitcast(I32), v_plane0[ROWS : ROWS + MOVED, :].bitcast(I32))
-        v_planes = (v_plane0, v_plane1)
-
-        w4_plane = held([P, PASSES, PACK, P], U8, "w4_plane")
-        nc.vector.tensor_copy(
-            w4_plane[:].rearrange("p a t m -> p a m t"),
-            w4_bytes[:].rearrange("p a (m t) -> p a m t", t=PACK),
         )
 
         v_words = {}
@@ -128,15 +141,95 @@ def tile_list_chiral_column_bench_kernel(
         gather_tab(0)
         v2_plane = held([P, S2], U8, "v2_plane")
         nc.vector.tensor_copy(v2_plane[:], tab2_bytes[:].indirect(idx2[:]))
+        w4_plane = held([P, PASSES, PACK, P], U8, "w4_plane")
+        nc.vector.tensor_copy(
+            w4_plane[:].rearrange("p a t m -> p a m t"),
+            w4_bytes[:].rearrange("p a (m t) -> p a m t", t=PACK),
+        )
         gather_tab(1)
 
-        w1_raw = []
-        for a in range(PASSES):
-            raw = held([P, PACK, H], F32, "w1_raw%d" % a, "slot%d" % a)
-            nc.sync.dma_start(raw[:], w1[a * P * PACK : (a + 1) * P * PACK, :].rearrange("(p j) c -> p j c", j=PACK))
-            w1_raw.append(raw)
-        tab2_tile = held([P, T2], U32, "tab2", "slot2")
+        load_w1(1, "slot0")
+        tab2_tile = held([P, T2], U32, "tab2", "slot1")
         nc.sync.dma_start(tab2_tile[:].bitcast(I32), tab2_words[0].rearrange("p t i -> p (t i)").bitcast(I32))
+
+        w1_codes, w1_planes = [], []
+
+        def quantise_w1(a, cast):
+            grouped = held([P, PACK * H], BF16, "w1_grouped%d" % a)
+            cast(
+                grouped[:].rearrange("p (t m j) -> p m j t", t=PACK, j=PACK),
+                w1_raw[a][:].rearrange("p j (m t) -> p m j t", t=PACK),
+            )
+            codes = held([P, H], U32, "w1_codes%d" % a)
+            plane = held([P, H], U8, "w1_plane%d" % a)
+            nc.vector.quantize_mx(out=codes[:].bitcast(FP8X4), scales=plane[:], in_=grouped[:])
+            w1_codes.append(codes)
+            w1_planes.append(plane)
+            return grouped
+
+        def res_pass(acc, half, t, a):
+            nc.tensor.matmul_mx(
+                acc[:], lhsT=w4_codes[:, a, t, :].bitcast(FP4X4), lhsT_scale=w4_plane[:, a, t, :],
+                rhs=v_words[a, half][:].bitcast(FP8X4), rhs_scale=v_planes[a][:, half * BANK : (half + 1) * BANK],
+                start=(a == 0), stop=(a == PASSES - 1),
+            )
+
+        def z_pass(acc, half, t, a):
+            wcols = slice(t * P, (t + 1) * P)
+            nc.tensor.matmul_mx(
+                acc[:], lhsT=w1_codes[a][:, wcols].bitcast(FP8X4), lhsT_scale=w1_planes[a][:, wcols],
+                rhs=v_words[a, half][:].bitcast(FP8X4), rhs_scale=v_planes[a][:, half * BANK : (half + 1) * BANK],
+                start=(a == 0), stop=(a == PASSES - 1),
+            )
+
+        def weigh_residual(acc, half, t):
+            res = held([P, BANK], F32, "res%d%d" % (half, t))
+            nc.scalar.activation(res[:], acc[:], ACT.Copy, scale=skip_c[:, t : t + 1])
+            return res
+
+        def combine(acc, res, rows4, t):
+            act = ring.tile([P, BANK], F32, name="act")
+            nc.scalar.activation(act[:], acc[:], ACT.Silu)
+            nc.vector.scalar_tensor_tensor(rows4[:, t, :], act[:], gain_c[:, t : t + 1], res[:], ALU.mult, ALU.add)
+
+        quantise_w1(0, nc.scalar.copy)
+        res_banks = [bank("res") for t in range(PACK)]
+        z_banks = [bank("z") for t in range(PACK)]
+        for t in range(PACK):
+            res_pass(res_banks[t], 0, t, 0)
+        for t in range(PACK):
+            z_pass(z_banks[t], 0, t, 0)
+        residuals = []
+        for t in range(PACK):
+            res_pass(res_banks[t], 0, t, 1)
+            residuals.append(weigh_residual(res_banks[t], 0, t))
+        grouped = quantise_w1(1, nc.vector.tensor_copy)
+
+        ref_tiles = []
+        for a in range(2):
+            given = held([P, TILES // 2, NP], F32, "ref%d" % a, "slot%d" % (2 - 2 * a))
+            rows = slice(a * S2 // 2, (a + 1) * S2 // 2)
+            nc.sync.dma_start(given[:], ref[rows, :].rearrange("(i p) n -> p i n", p=P))
+            ref_tiles.append(given)
+
+        v2_words = held([P, S2], U32, "v2_words")
+        nc.vector.tensor_copy(v2_words[:], tab2_tile[:].indirect(idx2[:]))
+
+        h_rows = [held([P, PACK, BANK], BF16, "h_rows%d" % half) for half in range(HALVES)]
+        for t in range(PACK):
+            z_pass(z_banks[t], 0, t, 1)
+            combine(z_banks[t], residuals[t], h_rows[0], t)
+        residuals = []
+        for t in range(PACK):
+            acc = bank("res")
+            for a in range(PASSES):
+                res_pass(acc, 1, t, a)
+            residuals.append(weigh_residual(acc, 1, t))
+        for t in range(PACK):
+            acc = bank("z")
+            for a in range(PASSES):
+                z_pass(acc, 1, t, a)
+            combine(acc, residuals[t], h_rows[1], t)
 
         turned = bank("turned", P)
         nc.tensor.transpose(turned[:], row_vectors[:], identity[:])
@@ -147,104 +240,66 @@ def tile_list_chiral_column_bench_kernel(
             gate_factor[:], col_vectors[:, 0:TILES], -1.0, col_vectors[:, TILES : 2 * TILES], ALU.mult, ALU.mult
         )
 
-        skipped = {}
-        for half in range(HALVES):
-            cols = slice(half * BANK, (half + 1) * BANK)
-            for t in range(PACK):
-                acc = bank("res")
-                for a in range(PASSES):
-                    nc.tensor.matmul_mx(
-                        acc[:], lhsT=w4_codes[:, a, t, :].bitcast(FP4X4), lhsT_scale=w4_plane[:, a, t, :],
-                        rhs=v_words[a, half][:].bitcast(FP8X4), rhs_scale=v_planes[a][:, cols],
-                        start=(a == 0), stop=(a == PASSES - 1),
-                    )
-                res = held([P, BANK], F32, "res%d%d" % (half, t))
-                nc.scalar.activation(res[:], acc[:], ACT.Copy, scale=skip_c[:, t : t + 1])
-                skipped[half, t] = res
-
-        w1_codes, w1_planes = [], []
-        for a in range(PASSES):
-            grouped = held([P, PACK * H], BF16, "w1_grouped%d" % a)
-            nc.vector.tensor_copy(
-                grouped[:].rearrange("p (t m j) -> p m j t", t=PACK, j=PACK),
-                w1_raw[a][:].rearrange("p j (m t) -> p m j t", t=PACK),
-            )
-            codes = held([P, H], U32, "w1_codes%d" % a)
-            plane = held([P, H], U8, "w1_plane%d" % a)
-            nc.vector.quantize_mx(out=codes[:].bitcast(FP8X4), scales=plane[:], in_=grouped[:])
-            w1_codes.append(codes)
-            w1_planes.append(plane)
-
-        ref_tiles = []
-        for a in range(2):
-            given = held([P, TILES // 2, NP], F32, "ref%d" % a, "slot%d" % a)
-            rows = slice(a * S2 // 2, (a + 1) * S2 // 2)
-            nc.sync.dma_start(given[:], ref[rows, :].rearrange("(i p) n -> p i n", p=P))
-            ref_tiles.append(given)
-
-        v2_words = held([P, S2], U32, "v2_words")
-        nc.vector.tensor_copy(v2_words[:], tab2_tile[:].indirect(idx2[:]))
-
-        h_rows, h_grouped = [], []
-        for half in range(HALVES):
-            cols = slice(half * BANK, (half + 1) * BANK)
-            rows4 = held([P, PACK, BANK], BF16, "h_rows%d" % half)
-            for t in range(PACK):
-                acc = bank("z")
-                wcols = slice(t * P, (t + 1) * P)
-                for a in range(PASSES):
-                    nc.tensor.matmul_mx(
-                        acc[:], lhsT=w1_codes[a][:, wcols].bitcast(FP8X4), lhsT_scale=w1_planes[a][:, wcols],
-                        rhs=v_words[a, half][:].bitcast(FP8X4), rhs_scale=v_planes[a][:, cols],
-                        start=(a == 0), stop=(a == PASSES - 1),
-                    )
-                act = ring.tile([P, BANK], F32, name="act")
-                nc.scalar.activation(act[:], acc[:], ACT.Silu)
-                nc.vector.scalar_tensor_tensor(
-                    rows4[:, t, :], act[:], gain_c[:, t : t + 1], skipped[half, t][:], ALU.mult, ALU.add
-                )
-            h_rows.append(rows4)
-
-        h_codes, h_planes = [], []
-        for half in range(HALVES):
-            grouped = held([P, PACK * BANK], BF16, "h_grouped%d" % half)
-            weave = nc.scalar.copy if half == 0 else nc.vector.tensor_copy
+        h_codes, h_planes, h_grouped = {}, {}, {}
+        for half, weave in ((0, nc.scalar.copy), (1, nc.scalar.copy)):
+            h_grouped[half] = held([P, PACK * BANK], BF16, "h_grouped%d" % half)
             weave(
-                grouped[:].rearrange("p (c i t) -> p c t i", i=4, t=PACK),
+                h_grouped[half][:].rearrange("p (c i t) -> p c t i", i=4, t=PACK),
                 h_rows[half][:].rearrange("p t (c i) -> p c t i", i=4),
             )
-            h_grouped.append(grouped)
-        for half in range(HALVES):
-            codes = held([P, BANK], U32, "h_codes%d" % half)
-            plane = held([P, BANK], U8, "h_plane%d" % half)
-            nc.vector.quantize_mx(out=codes[:].bitcast(FP8X4), scales=plane[:], in_=h_grouped[half][:])
-            h_codes.append(codes)
-            h_planes.append(plane)
+        h_grouped1 = h_grouped[1]
+
+        def quantise_h(half):
+            h_codes[half] = held([P, BANK], U32, "h_codes%d" % half)
+            h_planes[half] = held([P, BANK], U8, "h_plane%d" % half)
+            nc.vector.quantize_mx(out=h_codes[half][:].bitcast(FP8X4), scales=h_planes[half][:], in_=h_grouped[half][:])
+
+        def product(i, half):
+            acc = bank("e")
+            mcols = slice(i * P, (i + 1) * P)
+            nc.tensor.matmul_mx(
+                acc[:], lhsT=v2_words[:, mcols].bitcast(FP8X4), lhsT_scale=v2_plane[:, mcols],
+                rhs=h_codes[half][:].bitcast(FP8X4), rhs_scale=h_planes[half][:],
+                start=True, stop=True,
+            )
+            return acc
 
         top = held([P, TILES], F32, "top")
+        half_top = held([P, DIRECT], F32, "half_top")
         gate_bias = held([P, TILES], F32, "gate_bias")
-        floors, gates = [], []
+        floors, gates, direct = [], [], []
+        quantise_h(0)
+        for i in range(DIRECT):
+            scores = ring.tile([P, S], F32, name="scores", bufs=TILES)
+            nc.vector.tensor_scalar(
+                scores[:, 0:BANK], product(i, 0)[:], 1.0, None, ALU.mult, ALU.max, accum_out=half_top[:, i : i + 1]
+            )
+            direct.append(scores)
+        quantise_h(1)
 
         def finish(i):
             result = ring.tile([P, NP], F32, name="result")
-            nc.vector.scalar_tensor_tensor(
-                result[:], floors[i][:], col_vectors[:, 2 * TILES + i : 2 * TILES + i + 1], gates[i][:], ALU.mult, ALU.mult
-            )
+            weight = col_vectors[:, 2 * TILES + i : 2 * TILES + i + 1]
+            if i == TILES - 1:
+                nc.vector.scalar_tensor_tensor(result[:], floors[i][:], weight, gates[i][:], ALU.mult, ALU.mult)
+            else:
+                weighed = ring.tile([P, NP], F32, name="weighed")
+                nc.gpsimd.tensor_scalar(weighed[:], floors[i][:], weight, 0.0, ALU.mult, ALU.add)
+                nc.gpsimd.tensor_tensor(result[:], weighed[:], gates[i][:], ALU.mult)
             nc.sync.dma_start(out[i * P : (i + 1) * P, :], result[:])
 
         for i in range(TILES):
-            mcols = slice(i * P, (i + 1) * P)
             col = slice(i, i + 1)
-            scores = ring.tile([P, S], F32, name="scores")
-            for half in range(HALVES):
-                acc = bank("e")
-                nc.tensor.matmul_mx(
-                    acc[:], lhsT=v2_words[:, mcols].bitcast(FP8X4), lhsT_scale=v2_plane[:, mcols],
-                    rhs=h_codes[half][:].bitcast(FP8X4), rhs_scale=h_planes[half][:],
-                    start=True, stop=True,
+            if i < DIRECT:
+                scores = direct[i]
+                nc.vector.tensor_scalar(
+                    scores[:, BANK:S], product(i, 1)[:], 1.0, half_top[:, col], ALU.mult, ALU.max, accum_out=top[:, col]
                 )
-                nc.scalar.copy(scores[:, half * BANK : (half + 1) * BANK], acc[:])
-            nc.vector.tensor_reduce(top[:, col], scores[:], AXIS.X, ALU.max)
+            else:
+                scores = ring.tile([P, S], F32, name="scores", bufs=TILES)
+                for half in range(HALVES):
+                    nc.scalar.copy(scores[:, half * BANK : (half + 1) * BANK], product(i, half)[:])
+                nc.vector.tensor_reduce(top[:, col], scores[:], AXIS.X, ALU.max)
             picked = ring.tile([P, NP], F32, name="picked")
             nc.vector.tensor_copy(picked[:], scores[:].indirect(p2[:]))
             nc.scalar.activation(gate_bias[:, col], top[:, col], ACT.Copy, scale=gate_factor[:, col])
@@ -252,10 +307,8 @@ def tile_list_chiral_column_bench_kernel(
             nc.scalar.activation(
                 gate[:], scores[:].indirect(p1[:]), ACT.Sigmoid, bias=gate_bias[:, col], scale=col_vectors[:, col]
             )
-            if i > 0:
-                finish(i - 1)
             floored = ring.tile([P, NP], F32, name="floored")
             nc.vector.tensor_tensor(floored[:], picked[:], ref_tiles[i // 4][:, i % 4, :], ALU.max)
             floors.append(floored)
             gates.append(gate)
-        finish(TILES - 1)
+            finish(i)

@@ -26,9 +26,8 @@ HALVES = S // BANK
 TILES = S2 // P
 QUADS = 4
 ROWS = 4
-DEAD = 32 - PASSES * ROWS
 MOVED = 96 + ROWS
-DIRECT = 3
+DIRECT = 1
 
 
 def tile_list_chiral_column_bench_kernel(
@@ -48,21 +47,16 @@ def tile_list_chiral_column_bench_kernel(
         def bank(name, width=BANK):
             return psum.tile([P, width], F32, name=name, tag="bank")
 
-        tab2_bytes = held([P, T2], U8, "tab2_bytes", "slot1")
-        nc.gpsimd.memset(tab2_bytes[:].bitcast(I32), 0)
         w4_bytes = held([P, PASSES, H], U8, "w4_bytes")
         nc.gpsimd.memset(w4_bytes[:].bitcast(I32), 0)
-        tab_bytes = held([P, T], U8, "tab_bytes")
-        for q in range(QUADS):
-            clear = nc.vector.memset if q % 2 else nc.gpsimd.memset
-            clear(tab_bytes[32 * q : 32 * q + DEAD, :].bitcast(I32), 0)
+        tab2_bytes = held([P, T2], U8, "tab2_bytes", "slot1")
+        nc.gpsimd.memset(tab2_bytes[:].bitcast(I32), 0)
+        tab_bytes = held([P, T], U8, "tab_bytes", "slot0")
+        nc.vector.memset(tab_bytes[:].bitcast(I32), 0)
         row_vectors = held([P, P], F32, "row_vectors")
         nc.vector.memset(row_vectors[:], 0.0)
-        v_planes = []
-        for a in range(PASSES):
-            plane = held([P, S], U8, "v_plane%d" % a)
-            nc.vector.memset(plane[96:P, :].bitcast(I32), 0)
-            v_planes.append(plane)
+        moved_plane = held([P, S], U8, "moved_plane")
+        nc.vector.memset(moved_plane[96:P, :].bitcast(I32), 0)
 
         idx = lists.tile([P, S // 16], U16, name="idx")
         idx2 = lists.tile([P, S2 // 16], U16, name="idx2")
@@ -71,106 +65,103 @@ def tile_list_chiral_column_bench_kernel(
         tab_tiles = []
 
         def load_tab(a):
-            words = held([P, T], U32, "tab%d" % a, "slot0" if a == 0 else None)
+            words = held([P, T], U32, "tab%d" % a, "slot2" if a else None)
             nc.sync.dma_start(words[:].bitcast(I32), tab_words[a].rearrange("p t i -> p (t i)").bitcast(I32))
             tab_tiles.append(words)
 
         w1_raw = []
 
-        def load_w1(a, tag):
-            raw = held([P, PACK, H], F32, "w1_raw%d" % a, tag)
+        def load_w1(a):
+            raw = held([P, PACK, H], F32, "w1_raw%d" % a, "slot3" if a else None)
             nc.sync.dma_start(raw[:], w1[a * P * PACK : (a + 1) * P * PACK, :].rearrange("(p j) c -> p j c", j=PACK))
             w1_raw.append(raw)
 
-        nc.sync.dma_start(idx[:], offs)
         for q in range(QUADS):
-            nc.sync.dma_start(
-                tab_bytes[32 * q + DEAD : 32 * (q + 1), :].bitcast(I32),
+            nc.gpsimd.dma_start(
+                tab_bytes[32 * q : 32 * q + PASSES * ROWS, :].bitcast(I32),
                 tab_scales[:, ROWS * q : ROWS * (q + 1), :].bitcast(I32),
             )
         w4_raw = held([P, PASSES, 2 * H], U8, "w4_raw")
         nc.sync.dma_start(w4_raw[:].bitcast(I32), w4_words.rearrange("a p c -> p a c").bitcast(I32))
+        nc.sync.dma_start(idx[:], offs)
         load_tab(0)
+        for q in range(QUADS):
+            nc.sync.dma_start(
+                w4_bytes[32 * q : 32 * q + ROWS, :, :].bitcast(I32),
+                w4_scales[:, ROWS * q : ROWS * (q + 1), :].rearrange("a r c -> r a c").bitcast(I32),
+            )
+        load_w1(0)
         nc.sync.dma_start(idx2[:], offs2)
         for q in range(QUADS):
             nc.sync.dma_start(
                 tab2_bytes[32 * q : 32 * q + ROWS, :].bitcast(I32),
                 tab2_scales[0, ROWS * q : ROWS * (q + 1), :].bitcast(I32),
             )
-        load_w1(0, "slot2")
-        for q in range(QUADS):
-            nc.sync.dma_start(
-                w4_bytes[32 * q : 32 * q + ROWS, :, :].bitcast(I32),
-                w4_scales[:, ROWS * q : ROWS * (q + 1), :].rearrange("a r c -> r a c").bitcast(I32),
-            )
         load_tab(1)
-        nc.sync.dma_start(p1[:], pos1)
-        nc.sync.dma_start(p2[:], pos2)
         skip_c = held([P, PACK], F32, "skip_c")
         gain_c = held([P, PACK], F32, "gain_c")
+        nc.sync.dma_start(skip_c[:], skip.rearrange("(p t) -> p t", t=PACK))
+        nc.sync.dma_start(gain_c[:], gain.rearrange("(p t) -> p t", t=PACK))
+        load_w1(1)
+        tab2_tile = held([P, T2], U32, "tab2")
+        nc.sync.dma_start(tab2_tile[:].bitcast(I32), tab2_words[0].rearrange("p t i -> p (t i)").bitcast(I32))
+        nc.sync.dma_start(p1[:], pos1)
+        nc.sync.dma_start(p2[:], pos2)
+        for n, vec in enumerate((slope, share, rac)):
+            nc.sync.dma_start(row_vectors[TILES * n : TILES * (n + 1), :], vec.rearrange("(i p) -> i p", p=P))
+        ref_tiles = []
+        for a in range(2):
+            given = held([P, TILES // 2, NP], F32, "ref%d" % a)
+            rows = slice(a * S2 // 2, (a + 1) * S2 // 2)
+            nc.sync.dma_start(given[:], ref[rows, :].rearrange("(i p) n -> p i n", p=P))
+            ref_tiles.append(given)
         identity = held([P, P], F32, "identity")
         make_identity(nc, identity[:])
-        nc.gpsimd.dma_start(skip_c[:], skip.rearrange("(p t) -> p t", t=PACK))
-
-        v_bytes = held([P, S], U8, "v_bytes")
-        nc.vector.tensor_copy(v_bytes[:], tab_bytes[:].indirect(idx[:]))
-        for a in range(PASSES):
-            first = DEAD + a * ROWS
-            nc.gpsimd.dma_start(
-                v_planes[a][0:MOVED, :].bitcast(I32), v_bytes[first : first + MOVED, :].bitcast(I32)
-            )
-        nc.gpsimd.dma_start(gain_c[:], gain.rearrange("(p t) -> p t", t=PACK))
-        for n, vec in enumerate((slope, share, rac)):
-            nc.gpsimd.dma_start(row_vectors[TILES * n : TILES * (n + 1), :], vec.rearrange("(i p) -> i p", p=P))
 
         w4_codes = held([P, PASSES, PACK, 2 * P], U8, "w4_codes")
         nc.vector.tensor_copy(
-            w4_codes[:].rearrange("p a t (m b) -> p a m t b", b=2),
-            w4_raw[:].rearrange("p a (m t b) -> p a m t b", t=PACK, b=2),
+            w4_codes[:].rearrange("p a t (m b) -> p a t m b", b=2),
+            w4_raw[:].rearrange("p a (m t b) -> p a t m b", t=PACK, b=2),
         )
+        w4_plane = held([P, PASSES, PACK, P], U8, "w4_plane")
+        nc.vector.tensor_copy(w4_plane[:], w4_bytes[:].rearrange("p a (m t) -> p a t m", t=PACK))
 
-        v_words = {}
+        v_words = []
 
         def gather_tab(a):
+            picked = held([P, S], U32, "v_words%d" % a, "slot1" if a else None)
             for half in range(HALVES):
-                picked = held([P, BANK], U32, "v%d%d" % (a, half))
                 cols = slice(half * BANK // 16, (half + 1) * BANK // 16)
-                nc.vector.tensor_copy(picked[:], tab_tiles[a][:].indirect(idx[:, cols]))
-                v_words[a, half] = picked
+                nc.vector.tensor_copy(picked[:, half * BANK : (half + 1) * BANK], tab_tiles[a][:].indirect(idx[:, cols]))
+            v_words.append(picked)
 
         gather_tab(0)
-        v2_plane = held([P, S2], U8, "v2_plane")
+        v_bytes = held([P, S], U8, "v_bytes")
+        nc.vector.tensor_copy(v_bytes[:], tab_bytes[:].indirect(idx[:]))
+        nc.gpsimd.dma_start(moved_plane[0:MOVED, :].bitcast(I32), v_bytes[ROWS : ROWS + MOVED, :].bitcast(I32))
+        v_planes = [v_bytes, moved_plane]
+        v2_plane = held([P, S2], U8, "v2_plane", "slot0")
         nc.vector.tensor_copy(v2_plane[:], tab2_bytes[:].indirect(idx2[:]))
-        w4_plane = held([P, PASSES, PACK, P], U8, "w4_plane")
-        nc.vector.tensor_copy(
-            w4_plane[:].rearrange("p a t m -> p a m t"),
-            w4_bytes[:].rearrange("p a (m t) -> p a m t", t=PACK),
-        )
-        gather_tab(1)
-
-        load_w1(1, "slot0")
-        tab2_tile = held([P, T2], U32, "tab2", "slot1")
-        nc.sync.dma_start(tab2_tile[:].bitcast(I32), tab2_words[0].rearrange("p t i -> p (t i)").bitcast(I32))
 
         w1_codes, w1_planes = [], []
 
         def quantise_w1(a, cast):
-            grouped = held([P, PACK * H], BF16, "w1_grouped%d" % a)
+            grouped = held([P, PACK * H], BF16, "w1_grouped%d" % a, "slot2" if a else None)
             cast(
-                grouped[:].rearrange("p (t m j) -> p m j t", t=PACK, j=PACK),
-                w1_raw[a][:].rearrange("p j (m t) -> p m j t", t=PACK),
+                grouped[:].rearrange("p (t m j) -> p m t j", t=PACK, j=PACK),
+                w1_raw[a][:].rearrange("p j (m t) -> p m t j", t=PACK),
             )
             codes = held([P, H], U32, "w1_codes%d" % a)
             plane = held([P, H], U8, "w1_plane%d" % a)
             nc.vector.quantize_mx(out=codes[:].bitcast(FP8X4), scales=plane[:], in_=grouped[:])
             w1_codes.append(codes)
             w1_planes.append(plane)
-            return grouped
 
         def res_pass(acc, half, t, a):
             nc.tensor.matmul_mx(
                 acc[:], lhsT=w4_codes[:, a, t, :].bitcast(FP4X4), lhsT_scale=w4_plane[:, a, t, :],
-                rhs=v_words[a, half][:].bitcast(FP8X4), rhs_scale=v_planes[a][:, half * BANK : (half + 1) * BANK],
+                rhs=v_words[a][:, half * BANK : (half + 1) * BANK].bitcast(FP8X4),
+                rhs_scale=v_planes[a][:, half * BANK : (half + 1) * BANK],
                 start=(a == 0), stop=(a == PASSES - 1),
             )
 
@@ -178,7 +169,8 @@ def tile_list_chiral_column_bench_kernel(
             wcols = slice(t * P, (t + 1) * P)
             nc.tensor.matmul_mx(
                 acc[:], lhsT=w1_codes[a][:, wcols].bitcast(FP8X4), lhsT_scale=w1_planes[a][:, wcols],
-                rhs=v_words[a, half][:].bitcast(FP8X4), rhs_scale=v_planes[a][:, half * BANK : (half + 1) * BANK],
+                rhs=v_words[a][:, half * BANK : (half + 1) * BANK].bitcast(FP8X4),
+                rhs_scale=v_planes[a][:, half * BANK : (half + 1) * BANK],
                 start=(a == 0), stop=(a == PASSES - 1),
             )
 
@@ -193,43 +185,29 @@ def tile_list_chiral_column_bench_kernel(
             nc.vector.scalar_tensor_tensor(rows4[:, t, :], act[:], gain_c[:, t : t + 1], res[:], ALU.mult, ALU.add)
 
         quantise_w1(0, nc.scalar.copy)
-        res_banks = [bank("res") for t in range(PACK)]
-        z_banks = [bank("z") for t in range(PACK)]
-        for t in range(PACK):
-            res_pass(res_banks[t], 0, t, 0)
-        for t in range(PACK):
-            z_pass(z_banks[t], 0, t, 0)
-        residuals = []
-        for t in range(PACK):
-            res_pass(res_banks[t], 0, t, 1)
-            residuals.append(weigh_residual(res_banks[t], 0, t))
-        grouped = quantise_w1(1, nc.vector.tensor_copy)
+        res_banks = {(half, t): bank("res") for half in range(HALVES) for t in range(PACK)}
+        for half, t in res_banks:
+            acc = res_banks[half, t]
+            res_pass(acc, half, t, 0)
+        gather_tab(1)
+        residuals = {}
+        for half, t in res_banks:
+            acc = res_banks[half, t]
+            res_pass(acc, half, t, 1)
+            residuals[half, t] = weigh_residual(acc, half, t)
+        quantise_w1(1, nc.vector.tensor_copy)
 
-        ref_tiles = []
-        for a in range(2):
-            given = held([P, TILES // 2, NP], F32, "ref%d" % a, "slot%d" % (2 - 2 * a))
-            rows = slice(a * S2 // 2, (a + 1) * S2 // 2)
-            nc.sync.dma_start(given[:], ref[rows, :].rearrange("(i p) n -> p i n", p=P))
-            ref_tiles.append(given)
-
-        v2_words = held([P, S2], U32, "v2_words")
+        v2_words = held([P, S2], U32, "v2_words", "slot3")
         nc.vector.tensor_copy(v2_words[:], tab2_tile[:].indirect(idx2[:]))
 
         h_rows = [held([P, PACK, BANK], BF16, "h_rows%d" % half) for half in range(HALVES)]
-        for t in range(PACK):
-            z_pass(z_banks[t], 0, t, 1)
-            combine(z_banks[t], residuals[t], h_rows[0], t)
-        residuals = []
-        for t in range(PACK):
-            acc = bank("res")
-            for a in range(PASSES):
-                res_pass(acc, 1, t, a)
-            residuals.append(weigh_residual(acc, 1, t))
-        for t in range(PACK):
-            acc = bank("z")
-            for a in range(PASSES):
-                z_pass(acc, 1, t, a)
-            combine(acc, residuals[t], h_rows[1], t)
+        for half in range(HALVES):
+            z_banks = [bank("z") for t in range(PACK)]
+            for t in range(PACK):
+                z_pass(z_banks[t], half, t, 0)
+            for t in range(PACK):
+                z_pass(z_banks[t], half, t, 1)
+                combine(z_banks[t], residuals[half, t], h_rows[half], t)
 
         turned = bank("turned", P)
         nc.tensor.transpose(turned[:], row_vectors[:], identity[:])
@@ -241,13 +219,12 @@ def tile_list_chiral_column_bench_kernel(
         )
 
         h_codes, h_planes, h_grouped = {}, {}, {}
-        for half, weave in ((0, nc.scalar.copy), (1, nc.scalar.copy)):
+        for half, weave in ((0, nc.scalar.copy), (1, nc.vector.tensor_copy)):
             h_grouped[half] = held([P, PACK * BANK], BF16, "h_grouped%d" % half)
             weave(
                 h_grouped[half][:].rearrange("p (c i t) -> p c t i", i=4, t=PACK),
                 h_rows[half][:].rearrange("p t (c i) -> p c t i", i=4),
             )
-        h_grouped1 = h_grouped[1]
 
         def quantise_h(half):
             h_codes[half] = held([P, BANK], U32, "h_codes%d" % half)
@@ -268,24 +245,20 @@ def tile_list_chiral_column_bench_kernel(
         half_top = held([P, DIRECT], F32, "half_top")
         gate_bias = held([P, TILES], F32, "gate_bias")
         floors, gates, direct = [], [], []
-        quantise_h(0)
+        quantise_h(1)
         for i in range(DIRECT):
-            scores = ring.tile([P, S], F32, name="scores", bufs=TILES)
+            scores = ring.tile([P, S], F32, name="scores")
             nc.vector.tensor_scalar(
-                scores[:, 0:BANK], product(i, 0)[:], 1.0, None, ALU.mult, ALU.max, accum_out=half_top[:, i : i + 1]
+                scores[:, BANK:S], product(i, 1)[:], 1.0, None, ALU.mult, ALU.max, accum_out=half_top[:, i : i + 1]
             )
             direct.append(scores)
-        quantise_h(1)
+        quantise_h(0)
 
         def finish(i):
             result = ring.tile([P, NP], F32, name="result")
-            weight = col_vectors[:, 2 * TILES + i : 2 * TILES + i + 1]
-            if i == TILES - 1:
-                nc.vector.scalar_tensor_tensor(result[:], floors[i][:], weight, gates[i][:], ALU.mult, ALU.mult)
-            else:
-                weighed = ring.tile([P, NP], F32, name="weighed")
-                nc.gpsimd.tensor_scalar(weighed[:], floors[i][:], weight, 0.0, ALU.mult, ALU.add)
-                nc.gpsimd.tensor_tensor(result[:], weighed[:], gates[i][:], ALU.mult)
+            nc.vector.scalar_tensor_tensor(
+                result[:], floors[i][:], col_vectors[:, 2 * TILES + i : 2 * TILES + i + 1], gates[i][:], ALU.mult, ALU.mult
+            )
             nc.sync.dma_start(out[i * P : (i + 1) * P, :], result[:])
 
         for i in range(TILES):
@@ -293,11 +266,11 @@ def tile_list_chiral_column_bench_kernel(
             if i < DIRECT:
                 scores = direct[i]
                 nc.vector.tensor_scalar(
-                    scores[:, BANK:S], product(i, 1)[:], 1.0, half_top[:, col], ALU.mult, ALU.max, accum_out=top[:, col]
+                    scores[:, 0:BANK], product(i, 0)[:], 1.0, half_top[:, col], ALU.mult, ALU.max, accum_out=top[:, col]
                 )
             else:
-                scores = ring.tile([P, S], F32, name="scores", bufs=TILES)
-                for half in range(HALVES):
+                scores = ring.tile([P, S], F32, name="scores")
+                for half in (1, 0):
                     nc.scalar.copy(scores[:, half * BANK : (half + 1) * BANK], product(i, half)[:])
                 nc.vector.tensor_reduce(top[:, col], scores[:], AXIS.X, ALU.max)
             picked = ring.tile([P, NP], F32, name="picked")
@@ -307,8 +280,10 @@ def tile_list_chiral_column_bench_kernel(
             nc.scalar.activation(
                 gate[:], scores[:].indirect(p1[:]), ACT.Sigmoid, bias=gate_bias[:, col], scale=col_vectors[:, col]
             )
+            if i > 0:
+                finish(i - 1)
             floored = ring.tile([P, NP], F32, name="floored")
             nc.vector.tensor_tensor(floored[:], picked[:], ref_tiles[i // 4][:, i % 4, :], ALU.max)
             floors.append(floored)
             gates.append(gate)
-            finish(i)
+        finish(TILES - 1)

from contextlib import ExitStack

import concourse.mybir as mybir
from concourse.masks import make_identity

K, H, T, S, T2, S2, NP = 1024, 512, 4096, 1024, 2048, 1024, 512
FLOPS = 2 * K * H * S * 2 + 2 * H * S2 * S

F32 = mybir.dt.float32
BF16 = mybir.dt.bfloat16
I32 = mybir.dt.int32
U32 = mybir.dt.uint32
U16 = mybir.dt.uint16
U8 = mybir.dt.uint8
FP8X4 = mybir.dt.float8_e4m3fn_x4
FP4X4 = mybir.dt.float4_e2m1fn_x4
ALU = mybir.AluOpType
ACT = mybir.ActivationFunctionType
AXIS = mybir.AxisListType

P = 128
PACK = 4
PASSES = K // (P * PACK)
BANK = 512
HALVES = S // BANK
TILES = S2 // P
QUADS = 4
ROWS = 4
MOVED = 96 + ROWS
DIRECT = 1


def tile_list_chiral_column_bench_kernel(
    tc, tab_words, tab_scales, tab2_words, tab2_scales, offs, offs2, pos1, pos2,
    w1, w4_words, w4_scales, gain, skip, slope, share, ref, rac, out,
):
    nc = tc.nc
    with ExitStack() as ctx:
        lists = ctx.enter_context(tc.tile_pool(name="lists", bufs=1))
        keep = ctx.enter_context(tc.tile_pool(name="keep", bufs=1))
        ring = ctx.enter_context(tc.tile_pool(name="ring", bufs=4))
        psum = ctx.enter_context(tc.psum_pool(name="psum", bufs=8))

        def held(shape, dtype, name, tag=None):
            return keep.tile(shape, dtype, name=name, tag=tag or name, align_bytes=64)

        def bank(name, width=BANK):
            return psum.tile([P, width], F32, name=name, tag="bank")

        w4_bytes = held([P, PASSES, H], U8, "w4_bytes")
        nc.gpsimd.memset(w4_bytes[:].bitcast(I32), 0)
        tab2_bytes = held([P, T2], U8, "tab2_bytes", "slot1")
        nc.gpsimd.memset(tab2_bytes[:].bitcast(I32), 0)
        tab_bytes = held([P, T], U8, "tab_bytes", "slot0")
        nc.vector.memset(tab_bytes[:].bitcast(I32), 0)
        row_vectors = held([P, P], F32, "row_vectors")
        nc.vector.memset(row_vectors[:], 0.0)
        moved_plane = held([P, S], U8, "moved_plane")
        nc.vector.memset(moved_plane[96:P, :].bitcast(I32), 0)

        idx = lists.tile([P, S // 16], U16, name="idx")
        idx2 = lists.tile([P, S2 // 16], U16, name="idx2")
        p1 = lists.tile([P, NP // 16], U16, name="p1")
        p2 = lists.tile([P, NP // 16], U16, name="p2")
        tab_tiles = []

        def load_tab(a):
            words = held([P, T], U32, "tab%d" % a, "slot2" if a else None)
            nc.sync.dma_start(words[:].bitcast(I32), tab_words[a].rearrange("p t i -> p (t i)").bitcast(I32))
            tab_tiles.append(words)

        w1_raw = []

        def load_w1(a):
            raw = held([P, PACK, H], F32, "w1_raw%d" % a, "slot3" if a else None)
            nc.sync.dma_start(raw[:], w1[a * P * PACK : (a + 1) * P * PACK, :].rearrange("(p j) c -> p j c", j=PACK))
            w1_raw.append(raw)

        for q in range(QUADS):
            nc.gpsimd.dma_start(
                tab_bytes[32 * q : 32 * q + PASSES * ROWS, :].bitcast(I32),
                tab_scales[:, ROWS * q : ROWS * (q + 1), :].bitcast(I32),
            )
        w4_raw = held([P, PASSES, 2 * H], U8, "w4_raw")
        nc.sync.dma_start(w4_raw[:].bitcast(I32), w4_words.rearrange("a p c -> p a c").bitcast(I32))
        nc.sync.dma_start(idx[:], offs)
        load_tab(0)
        for q in range(QUADS):
            nc.sync.dma_start(
                w4_bytes[32 * q : 32 * q + ROWS, :, :].bitcast(I32),
                w4_scales[:, ROWS * q : ROWS * (q + 1), :].rearrange("a r c -> r a c").bitcast(I32),
            )
        load_w1(0)
        nc.sync.dma_start(idx2[:], offs2)
        for q in range(QUADS):
            nc.sync.dma_start(
                tab2_bytes[32 * q : 32 * q + ROWS, :].bitcast(I32),
                tab2_scales[0, ROWS * q : ROWS * (q + 1), :].bitcast(I32),
            )
        load_tab(1)
        skip_c = held([P, PACK], F32, "skip_c")
        gain_c = held([P, PACK], F32, "gain_c")
        nc.sync.dma_start(skip_c[:], skip.rearrange("(p t) -> p t", t=PACK))
        nc.sync.dma_start(gain_c[:], gain.rearrange("(p t) -> p t", t=PACK))
        load_w1(1)
        tab2_tile = held([P, T2], U32, "tab2")
        nc.sync.dma_start(tab2_tile[:].bitcast(I32), tab2_words[0].rearrange("p t i -> p (t i)").bitcast(I32))
        nc.sync.dma_start(p1[:], pos1)
        nc.sync.dma_start(p2[:], pos2)
        for n, vec in enumerate((slope, share, rac)):
            nc.sync.dma_start(row_vectors[TILES * n : TILES * (n + 1), :], vec.rearrange("(i p) -> i p", p=P))
        ref_tiles = []
        for a in range(2):
            given = held([P, TILES // 2, NP], F32, "ref%d" % a)
            rows = slice(a * S2 // 2, (a + 1) * S2 // 2)
            nc.sync.dma_start(given[:], ref[rows, :].rearrange("(i p) n -> p i n", p=P))
            ref_tiles.append(given)
        identity = held([P, P], F32, "identity")
        make_identity(nc, identity[:])

        w4_codes = held([P, PASSES, PACK, 2 * P], U8, "w4_codes")
        nc.vector.tensor_copy(
            w4_codes[:].rearrange("p a t (m b) -> p a t m b", b=2),
            w4_raw[:].rearrange("p a (m t b) -> p a t m b", t=PACK, b=2),
        )
        w4_plane = held([P, PASSES, PACK, P], U8, "w4_plane")
        nc.vector.tensor_copy(w4_plane[:], w4_bytes[:].rearrange("p a (m t) -> p a t m", t=PACK))

        v_words = []

        def gather_tab(a):
            picked = held([P, S], U32, "v_words%d" % a, "slot1" if a else None)
            for half in range(HALVES):
                cols = slice(half * BANK // 16, (half + 1) * BANK // 16)
                nc.vector.tensor_copy(picked[:, half * BANK : (half + 1) * BANK], tab_tiles[a][:].indirect(idx[:, cols]))
            v_words.append(picked)

        gather_tab(0)
        v_bytes = held([P, S], U8, "v_bytes")
        nc.vector.tensor_copy(v_bytes[:], tab_bytes[:].indirect(idx[:]))
        nc.gpsimd.dma_start(moved_plane[0:MOVED, :].bitcast(I32), v_bytes[ROWS : ROWS + MOVED, :].bitcast(I32))
        v_planes = [v_bytes, moved_plane]
        v2_plane = held([P, S2], U8, "v2_plane", "slot0")
        nc.vector.tensor_copy(v2_plane[:], tab2_bytes[:].indirect(idx2[:]))

        w1_codes, w1_planes = [], []

        def quantise_w1(a, cast):
            grouped = held([P, PACK * H], BF16, "w1_grouped%d" % a, "slot2" if a else None)
            cast(
                grouped[:].rearrange("p (t m j) -> p m t j", t=PACK, j=PACK),
                w1_raw[a][:].rearrange("p j (m t) -> p m t j", t=PACK),
            )
            codes = held([P, H], U32, "w1_codes%d" % a)
            plane = held([P, H], U8, "w1_plane%d" % a)
            nc.vector.quantize_mx(out=codes[:].bitcast(FP8X4), scales=plane[:], in_=grouped[:])
            w1_codes.append(codes)
            w1_planes.append(plane)

        def res_pass(acc, half, t, a):
            nc.tensor.matmul_mx(
                acc[:], lhsT=w4_codes[:, a, t, :].bitcast(FP4X4), lhsT_scale=w4_plane[:, a, t, :],
                rhs=v_words[a][:, half * BANK : (half + 1) * BANK].bitcast(FP8X4),
                rhs_scale=v_planes[a][:, half * BANK : (half + 1) * BANK],
                start=(a == 0), stop=(a == PASSES - 1),
            )

        def z_pass(acc, half, t, a):
            wcols = slice(t * P, (t + 1) * P)
            nc.tensor.matmul_mx(
                acc[:], lhsT=w1_codes[a][:, wcols].bitcast(FP8X4), lhsT_scale=w1_planes[a][:, wcols],
                rhs=v_words[a][:, half * BANK : (half + 1) * BANK].bitcast(FP8X4),
                rhs_scale=v_planes[a][:, half * BANK : (half + 1) * BANK],
                start=(a == 0), stop=(a == PASSES - 1),
            )

        def weigh_residual(acc, half, t):
            res = held([P, BANK], F32, "res%d%d" % (half, t))
            nc.scalar.activation(res[:], acc[:], ACT.Copy, scale=skip_c[:, t : t + 1])
            return res

        def combine(acc, res, rows4, t):
            act = ring.tile([P, BANK], F32, name="act")
            nc.scalar.activation(act[:], acc[:], ACT.Silu)
            nc.vector.scalar_tensor_tensor(rows4[:, t, :], act[:], gain_c[:, t : t + 1], res[:], ALU.mult, ALU.add)

        quantise_w1(0, nc.scalar.copy)
        res_banks = {(half, t): bank("res") for half in range(HALVES) for t in range(PACK)}
        for half, t in res_banks:
            acc = res_banks[half, t]
            res_pass(acc, half, t, 0)
        gather_tab(1)
        residuals = {}
        for half, t in res_banks:
            acc = res_banks[half, t]
            res_pass(acc, half, t, 1)
            residuals[half, t] = weigh_residual(acc, half, t)
        quantise_w1(1, nc.vector.tensor_copy)

        v2_words = held([P, S2], U32, "v2_words", "slot3")
        nc.vector.tensor_copy(v2_words[:], tab2_tile[:].indirect(idx2[:]))

        h_rows = [held([P, PACK, BANK], BF16, "h_rows%d" % half) for half in range(HALVES)]
        for half in range(HALVES):
            z_banks = [bank("z") for t in range(PACK)]
            for t in range(PACK):
                z_pass(z_banks[t], half, t, 0)
            for t in range(PACK):
                z_pass(z_banks[t], half, t, 1)
                combine(z_banks[t], residuals[half, t], h_rows[half], t)

        turned = bank("turned", P)
        nc.tensor.transpose(turned[:], row_vectors[:], identity[:])
        col_vectors = held([P, 3 * TILES], F32, "col_vectors")
        nc.scalar.copy(col_vectors[:], turned[:, 0 : 3 * TILES])
        gate_factor = held([P, TILES], F32, "gate_factor")
        nc.vector.scalar_tensor_tensor(
            gate_factor[:], col_vectors[:, 0:TILES], -1.0, col_vectors[:, TILES : 2 * TILES], ALU.mult, ALU.mult
        )

        h_codes, h_planes, h_grouped = {}, {}, {}
        for half, weave in ((0, nc.scalar.copy), (1, nc.vector.tensor_copy)):
            h_grouped[half] = held([P, PACK * BANK], BF16, "h_grouped%d" % half)
            weave(
                h_grouped[half][:].rearrange("p (c i t) -> p c t i", i=4, t=PACK),
                h_rows[half][:].rearrange("p t (c i) -> p c t i", i=4),
            )

        def quantise_h(half):
            h_codes[half] = held([P, BANK], U32, "h_codes%d" % half)
            h_planes[half] = held([P, BANK], U8, "h_plane%d" % half)
            nc.vector.quantize_mx(out=h_codes[half][:].bitcast(FP8X4), scales=h_planes[half][:], in_=h_grouped[half][:])

        def product(i, half):
            acc = bank("e")
            mcols = slice(i * P, (i + 1) * P)
            nc.tensor.matmul_mx(
                acc[:], lhsT=v2_words[:, mcols].bitcast(FP8X4), lhsT_scale=v2_plane[:, mcols],
                rhs=h_codes[half][:].bitcast(FP8X4), rhs_scale=h_planes[half][:],
                start=True, stop=True,
            )
            return acc

        top = held([P, TILES], F32, "top")
        half_top = held([P, DIRECT], F32, "half_top")
        gate_bias = held([P, TILES], F32, "gate_bias")
        floors, gates, direct = [], [], []
        quantise_h(1)
        for i in range(DIRECT):
            scores = ring.tile([P, S], F32, name="scores")
            nc.vector.tensor_scalar(
                scores[:, BANK:S], product(i, 1)[:], 1.0, None, ALU.mult, ALU.max, accum_out=half_top[:, i : i + 1]
            )
            direct.append(scores)
        quantise_h(0)

        def finish(i):
            result = ring.tile([P, NP], F32, name="result")
            nc.vector.scalar_tensor_tensor(
                result[:], floors[i][:], col_vectors[:, 2 * TILES + i : 2 * TILES + i + 1], gates[i][:], ALU.mult, ALU.mult
            )
            nc.sync.dma_start(out[i * P : (i + 1) * P, :], result[:])

        for i in range(TILES):
            col = slice(i, i + 1)
            if i < DIRECT:
                scores = direct[i]
                nc.vector.tensor_scalar(
                    scores[:, 0:BANK], product(i, 0)[:], 1.0, half_top[:, col], ALU.mult, ALU.max, accum_out=top[:, col]
                )
            else:
                scores = ring.tile([P, S], F32, name="scores")
                for half in (1, 0):
                    nc.scalar.copy(scores[:, half * BANK : (half + 1) * BANK], product(i, half)[:])
                nc.vector.tensor_reduce(top[:, col], scores[:], AXIS.X, ALU.max)
            picked = ring.tile([P, NP], F32, name="picked")
            nc.vector.tensor_copy(picked[:], scores[:].indirect(p2[:]))
            nc.scalar.activation(gate_bias[:, col], top[:, col], ACT.Copy, scale=gate_factor[:, col])
            gate = ring.tile([P, NP], F32, name="gate")
            nc.scalar.activation(
                gate[:], scores[:].indirect(p1[:]), ACT.Sigmoid, bias=gate_bias[:, col], scale=col_vectors[:, col]
            )
            if i > 0:
                finish(i - 1)
            floored = ring.tile([P, NP], F32, name="floored")
            nc.vector.tensor_tensor(floored[:], picked[:], ref_tiles[i // 4][:, i % 4, :], ALU.max)
            floors.append(floored)
            gates.append(gate)
        finish(TILES - 1)
